import numpy as np
import ml_dtypes


def mxq(x, axis, fmt="e4m3"):
    dtype, down = {"e4m3": (ml_dtypes.float8_e4m3fn, 7), "e5m2": (ml_dtypes.float8_e5m2, 14)}[fmt]
    v = np.moveaxis(np.asarray(x, np.float32).astype(ml_dtypes.bfloat16).astype(np.float64), axis, -1)
    blocks = v.reshape(v.shape[:-1] + (-1, 32))
    amax = np.abs(blocks).max(-1, keepdims=True)
    byte = np.maximum(np.where(amax > 0, np.frexp(amax)[1] - 1 + 127, 0) - down, 1)
    scale = np.exp2(byte - 127.0)
    codes = (blocks / scale).astype(np.float32).astype(dtype).astype(np.float64)
    return np.moveaxis((codes * scale).reshape(v.shape), -1, axis)


WIDE = False


def mx_kscale(k):
    if not WIDE:
        return np.ones(k)
    levels = np.array([10, -10, 5, -5, 0])
    if k % 512:
        return np.exp2(np.random.permutation(np.resize(levels, k // 32))).repeat(32)
    a = np.empty((k // 512, 16))
    for p in range(k // 512):
        a[p, :8] = np.random.permutation(np.resize(levels, 8))
        for g in range(8):
            far = levels[np.abs(levels - a[p, g]) >= 10]
            a[p, g + 8] = far[np.random.randint(len(far))]
    return np.exp2(a.ravel()).repeat(32)


def f64(x):
    return np.asarray(x).astype(np.float64)


def striped(idx):
    return np.tile(np.asarray(idx).reshape(-1, 16).T, (8, 1)).astype(np.uint16)


def unstriped(offs):
    return offs[:16].T.reshape(-1).astype(np.int64)


E2M1 = np.array([0.0, 0.5, 1.0, 1.5, 2.0, 3.0, 4.0, 6.0, -0.0, -0.5, -1.0, -1.5, -2.0, -3.0, -4.0, -6.0])


def pack_weight(w, fmt):
    k, n = w.shape
    w = f64(np.asarray(w, np.float32).astype(ml_dtypes.bfloat16)).reshape(k // 32, 32, n)
    amax = np.abs(w).max(1)
    if fmt == "e4m3":
        byte = np.frexp(amax)[1] - 1 + 127 - 7
    else:
        mant, ex = np.frexp(amax / 6.0)
        byte = np.where(mant > 0.5, ex, ex - 1) + 127
    byte = np.clip(np.where(amax > 0, byte, 1), 1, 254)
    scaled = (w * np.exp2(127.0 - byte)[:, None, :]).reshape(k, n).astype(np.float32)
    by_word = np.ascontiguousarray(scaled.reshape(k // 512, 128, 4, n).transpose(0, 1, 3, 2))
    if fmt == "e4m3":
        words = by_word.astype(ml_dtypes.float8_e4m3fn).view(np.uint8)
    else:
        c = by_word.astype(ml_dtypes.float4_e2m1fn).view(np.uint8) & 0xF
        words = (c[..., 0::2] | (c[..., 1::2] << 4)).reshape(k // 512, 128, 2 * n)
    return np.ascontiguousarray(words), np.ascontiguousarray(byte.astype(np.uint8).reshape(k // 512, 16, n))


def unpack_weight(words, scales, fmt):
    g, _, n = scales.shape
    words = np.ascontiguousarray(words).reshape(g, 128, n, -1)
    if fmt == "e4m3":
        vals = words.view(ml_dtypes.float8_e4m3fn).astype(np.float64)
    else:
        nib = np.empty((g, 128, n, 4), np.uint8)
        nib[..., 0::2] = words & 0xF
        nib[..., 1::2] = words >> 4
        vals = E2M1[nib]
    vals = vals * np.repeat(np.exp2(scales.astype(np.float64) - 127.0), 8, axis=1)[..., None]
    return vals.transpose(0, 1, 3, 2).reshape(g * 512, n)


def sigmoid(v):
    return 1.0 / (1.0 + np.exp(-v))


D, E, T, I, Q, G = 512, 512, 2048, 512, 128, 32


def setup_inputs():
    n = np.random.standard_normal
    idx = np.random.permutation(T)[:I]
    fd = mx_kscale(D)
    fe = mx_kscale(E)
    keysp = pack_weight(n((D, T)) / fd[:, None], "e2m1")
    valsp = pack_weight(n((E, T)) / fe[:, None], "e2m1")
    return {
        "query": (n((D, Q)) * 0.8 / np.sqrt(D) * fd[:, None]).astype(np.float32),
        "keys_words": keysp[0],
        "keys_scales": keysp[1],
        "th": (np.random.uniform(-0.5, 0.5, (Q, 1))).astype(np.float32),
        "sharp": (np.random.uniform(1.0, 3.0, (Q, 1))).astype(np.float32),
        "gout": (n((E, Q)) * 1 / np.sqrt(E) * fe[:, None]).astype(np.float32),
        "vals_words": valsp[0],
        "vals_scales": valsp[1],
        "base": (0.5 * n((Q, I))).astype(np.float32),
        "offs": striped(idx),
    }


def reference(query, keys_words, keys_scales, th, sharp, gout, vals_words, vals_scales, base, offs):
    idx = unstriped(offs)
    keysu = unpack_weight(keys_words, keys_scales, "e2m1")
    valsu = unpack_weight(vals_words, vals_scales, "e2m1")
    queryq = mxq(f64(query), 0, "e4m3")
    keysidxg = keysu[:, idx]
    a = queryq.T @ keysidxg
    s = a.reshape(Q, G, I // G).mean(axis=2) * f64(sharp)
    p = np.exp(s - np.max(s, axis=1, keepdims=True))
    z = np.sum(p, axis=1, keepdims=True)
    r = p / z
    rr = np.repeat(r, I // G, axis=1)
    goutq = mxq(f64(gout), 0, "e4m3")
    valsidxg = valsu[:, idx]
    c0 = goutq.T @ valsidxg
    drr = c0 * sigmoid(a - f64(th))
    dr = drr.reshape(Q, G, I // G).sum(axis=2)
    dz = np.sum(dr * p / np.square(z) * (-1.0), axis=1, keepdims=True)
    dp = dr / z + dz
    ds = dp * p
    e1 = ds * f64(sharp) / 16.0
    r1 = np.repeat(e1, I // G, axis=1)
    da = c0 * rr * sigmoid(a - f64(th)) * (1.0 - sigmoid(a - f64(th))) + r1
    hda = da * 32.0 * 2.0 * 32.0
    he1 = hda.reshape(Q, G, I // G).sum(axis=2)
    hds = he1 / 16.0 * f64(sharp)
    hdp = hds * p
    hdz = np.sum(hdp, axis=1, keepdims=True)
    hdr = hdp / z + hdz * (-1.0) / np.square(z) * p
    r51 = np.repeat(hdr, I // G, axis=1)
    hrr = hda * (1.0 - sigmoid(a - f64(th))) * sigmoid(a - f64(th)) * c0
    hr = hrr.reshape(Q, G, I // G).sum(axis=2)
    hz = np.sum(hdp * dr / np.square(z) * (-1.0), axis=1, keepdims=True) + np.sum(hdz * (-1.0) * dr * p / np.square(np.square(z)) * (-1.0), axis=1, keepdims=True) * z * 2.0 + np.sum(hr * p / np.square(z) * (-1.0), axis=1, keepdims=True)
    hp = hds * dp + hdz * (-1.0) / np.square(z) * dr + hr / z + hz
    hs = hp * p
    e52 = hs * f64(sharp) / 16.0
    r52 = np.repeat(e52, I // G, axis=1)
    ha = hda * (1.0 - sigmoid(a - f64(th))) * c0 * rr * sigmoid(a - f64(th)) * (1.0 - sigmoid(a - f64(th))) + hda * c0 * rr * sigmoid(a - f64(th)) * (-1.0) * sigmoid(a - f64(th)) * (1.0 - sigmoid(a - f64(th))) + r51 * c0 * sigmoid(a - f64(th)) * (1.0 - sigmoid(a - f64(th))) + r52
    y = ha + f64(base)
    return y

@@ -1,0 +1,235 @@
+from contextlib import ExitStack
+
+import concourse.mybir as mybir
+
+F32 = mybir.dt.float32
+BF16 = mybir.dt.bfloat16
+I32 = mybir.dt.int32
+U32 = mybir.dt.uint32
+U16 = mybir.dt.uint16
+U8 = mybir.dt.uint8
+FP8X4 = mybir.dt.float8_e4m3fn_x4
+FP4X4 = mybir.dt.float4_e2m1fn_x4
+ALU = mybir.AluOpType
+ACT = mybir.ActivationFunctionType
+AX = mybir.AxisListType
+
+P = 128
+PACK = 4
+TOKENS = 2048
+SLOTS = 512
+PAGES = 32
+PAGE = 16
+HALVES = 2
+
+FLOPS = 2 * 2 * 512 * P * SLOTS
+
+
+def tile_attend_gppagetimessigmoid_kernel(
+    tc, query, keys_words, keys_scales, th, sharp, gout, vals_words, vals_scales, base, offs, out
+):
+    nc = tc.nc
+    with ExitStack() as ctx:
+        pool = ctx.enter_context(tc.tile_pool(name="sbuf", bufs=1))
+        psum = ctx.enter_context(tc.psum_pool(name="psum", bufs=1))
+
+        def f32(width, name):
+            return pool.tile([P, width], F32, name=name)
+
+        def paged(ap):
+            return ap.rearrange("p (g j) -> p g j", j=PAGE)
+
+        def spread(ap):
+            return ap.unsqueeze(2).to_broadcast([P, ap.shape[1], PAGE])
+
+        offsets = pool.tile([P, SLOTS // 16], U16, name="offsets")
+        nc.sync.dma_start(offsets[:], offs)
+
+        def load_words(words, name):
+            tile = pool.tile([P, TOKENS], U16, name=name, tag=name)
+            nc.sync.dma_start(tile[:].bitcast(I32), words[0].bitcast(I32))
+            return tile
+
+        def load_scales(clear, queue, scales, name):
+            tile = pool.tile([P, TOKENS], U8, name=name)
+            clear.memset(tile[:].bitcast(I32), 0)
+            for quad in range(4):
+                queue.dma_start(
+                    tile[32 * quad : 32 * quad + 4, :].bitcast(I32),
+                    scales[0, 4 * quad : 4 * quad + 4, :].bitcast(I32),
+                )
+            return tile
+
+        def load_rows(rows, name):
+            raw = pool.tile([P, PACK, P], F32, name=name, tag=name)
+            nc.sync.dma_start(raw[:], rows.rearrange("(p j) q -> p j q", j=PACK))
+            return raw
+
+        def interleave(raw, name):
+            grouped = pool.tile([P, P, PACK], BF16, name=name, align_bytes=64)
+            nc.scalar.copy(grouped[:], raw[:].rearrange("p j q -> p q j"))
+            return grouped
+
+        def quantise(grouped, name):
+            codes = pool.tile([P, P], U32, name=name + "_codes", align_bytes=64)
+            scales = pool.tile([P, P], U8, name=name + "_scales", align_bytes=64)
+            nc.vector.quantize_mx(
+                out=codes[:].bitcast(FP8X4),
+                scales=scales[:],
+                in_=grouped[:].rearrange("p q j -> p (q j)"),
+            )
+            return codes, scales
+
+        def gather(window, entries, dtype, name):
+            picked = pool.tile([P, 16 * entries.shape[1]], dtype, name=name, align_bytes=64)
+            nc.vector.tensor_copy(picked[:], window[:].indirect(entries))
+            return picked
+
+        def product(codes, scales, words, word_scales, name):
+            acc = psum.tile([P, words.shape[1]], F32, name=name)
+            nc.tensor.matmul_mx(
+                out=acc[:],
+                lhsT=codes[:].bitcast(FP8X4),
+                lhsT_scale=scales[:],
+                rhs=words.bitcast(FP4X4),
+                rhs_scale=word_scales,
+                start=True,
+                stop=True,
+            )
+            return acc
+
+        key_scale_pool = load_scales(nc.vector, nc.scalar, keys_scales, "key_scale_pool")
+        key_word_pool = load_words(keys_words, "key_word_pool")
+        query_raw = load_rows(query, "query_raw")
+        val_word_pool = load_words(vals_words, "val_word_pool")
+
+        th_col = f32(1, "th_col")
+        nc.gpsimd.dma_start(th_col[:], th)
+        sharp_col = f32(1, "sharp_col")
+        nc.gpsimd.dma_start(sharp_col[:], sharp)
+
+        val_scale_pool = load_scales(nc.gpsimd, nc.sync, vals_scales, "val_scale_pool")
+
+        warm = pool.tile([P, 1], F32, name="warm", tag="gout_raw")
+        nc.vector.memset(warm[:], 0.0)
+        warm_out = f32(1, "warm_out")
+        nc.scalar.activation(warm_out[:], warm[:], ACT.Exp)
+
+        query_grouped = interleave(query_raw, "query_grouped")
+        gout_raw = load_rows(gout, "gout_raw")
+
+        key_scales = gather(key_scale_pool, offsets[:], U8, "key_scales")
+        key_words = gather(key_word_pool, offsets[:], U16, "key_words")
+        q_codes, q_scales = quantise(query_grouped, "query")
+        a = product(q_codes, q_scales, key_words[:], key_scales[:], "a")
+
+        base_sb = pool.tile([P, SLOTS], F32, name="base_sb", tag="key_word_pool")
+        nc.sync.dma_start(base_sb[:], base)
+
+        def row_factor(col, factor, name):
+            tile = f32(1, name)
+            nc.scalar.mul(tile[:], col[:], factor)
+            return tile
+
+        th_bias = row_factor(th_col, -0.5, "th_bias")
+        neg_k = row_factor(sharp_col, -1.0 / 16.0, "neg_k")
+        kappa_k = row_factor(sharp_col, -1.0 / 8.0, "kappa_k")
+        r3_k = row_factor(sharp_col, 8.0, "r3_k")
+        g_k = row_factor(sharp_col, 128.0, "g_k")
+
+        gout_grouped = interleave(gout_raw, "gout_grouped")
+        val_words = gather(val_word_pool, offsets[:], U16, "val_words")
+        g_codes, g_scales = quantise(gout_grouped, "gout")
+        width = SLOTS // HALVES
+        c = []
+        for half in range(HALVES):
+            cols = slice(half * width, (half + 1) * width)
+            pages = slice(half * PAGES // HALVES, (half + 1) * PAGES // HALVES)
+            val_scales = gather(val_scale_pool, offsets[:, pages], U8, "val_scales_%d" % half)
+            c.append(product(g_codes, g_scales, val_words[:, cols], val_scales[:], "c_%d" % half))
+
+        t = f32(SLOTS, "t")
+        nc.scalar.activation(t[:], a[:], ACT.Tanh, bias=th_bias[:], scale=0.5)
+        tt = f32(SLOTS, "tt")
+        nc.scalar.activation(tt[:], t[:], ACT.Square)
+
+        a_sum = f32(PAGES, "a_sum")
+        nc.vector.tensor_reduce(a_sum[:], paged(a[:]), AX.X, ALU.add)
+        neg_s = f32(PAGES, "neg_s")
+        neg_max = f32(1, "neg_max")
+        nc.vector.tensor_scalar(neg_s[:], a_sum[:], neg_k[:], None, ALU.mult, ALU.min, accum_out=neg_max[:])
+        p = f32(PAGES, "p")
+        z = f32(1, "z")
+        nc.scalar.activation(p[:], neg_s[:], ACT.Exp, bias=neg_max[:], scale=-1.0, accum_out=z[:])
+        inv_z = f32(1, "inv_z")
+        nc.vector.reciprocal(inv_z[:], z[:])
+        r = f32(PAGES, "r")
+        nc.scalar.activation(r[:], p[:], ACT.Identity, scale=inv_z[:])
+        r2 = f32(PAGES, "r2")
+        nc.scalar.activation(r2[:], p[:], ACT.Square, scale=inv_z[:])
+        r3 = f32(PAGES, "r3")
+        nc.scalar.activation(r3[:], r2[:], ACT.Identity, scale=r3_k[:])
+
+        u = f32(SLOTS, "u")
+        w = f32(SLOTS, "w")
+        for half in range(HALVES):
+            cols = slice(half * width, (half + 1) * width)
+            nc.vector.scalar_tensor_tensor(w[:, cols], t[:, cols], 1.0, c[half][:], ALU.add, ALU.mult)
+            nc.vector.scalar_tensor_tensor(u[:, cols], tt[:, cols], -1.0, c[half][:], ALU.add, ALU.mult)
+        uu = f32(SLOTS, "uu")
+        nc.scalar.activation(uu[:], u[:], ACT.Square)
+
+        w_sum = f32(PAGES, "w_sum")
+        nc.vector.tensor_reduce(w_sum[:], paged(w[:]), AX.X, ALU.add)
+        rw = f32(PAGES, "rw")
+        w_mean = f32(1, "w_mean")
+        nc.vector.scalar_tensor_tensor(rw[:], w_sum[:], 1.0, r[:], ALU.mult, ALU.mult, accum_out=w_mean[:])
+        kappa = f32(PAGES, "kappa")
+        nc.vector.tensor_scalar(kappa[:], w_sum[:], w_mean[:], kappa_k[:], ALU.subtract, ALU.mult)
+        beta = f32(PAGES, "beta")
+        nc.vector.tensor_tensor(beta[:], kappa[:], r2[:], ALU.mult)
+
+        lin = f32(SLOTS, "lin")
+        for g in range(PAGES):
+            cols = slice(g * PAGE, (g + 1) * PAGE)
+            nc.scalar.activation(
+                lin[:, cols], u[:, cols], ACT.Identity, bias=beta[:, g : g + 1], scale=r2[:, g : g + 1]
+            )
+
+        u_sum = f32(PAGES, "u_sum")
+        nc.vector.tensor_reduce(u_sum[:], paged(u[:]), AX.X, ALU.add)
+        ru = f32(PAGES, "ru")
+        nc.vector.tensor_tensor(ru[:], u_sum[:], r3[:], ALU.mult)
+        g1 = f32(PAGES, "g1")
+        g_sum = f32(1, "g_sum")
+        nc.vector.scalar_tensor_tensor(g1[:], beta[:], g_k[:], ru[:], ALU.mult, ALU.add, accum_out=g_sum[:])
+        hn = f32(PAGES, "hn")
+        nc.vector.scalar_tensor_tensor(hn[:], r[:], g_sum[:], g1[:], ALU.mult, ALU.subtract)
+        p1 = f32(PAGES, "p1")
+        nc.vector.tensor_tensor(p1[:], hn[:], ru[:], ALU.subtract)
+        p2 = f32(PAGES, "p2")
+        nc.vector.tensor_tensor(p2[:], p1[:], kappa[:], ALU.mult)
+        uu_sum = f32(PAGES, "uu_sum")
+        nc.vector.tensor_reduce(uu_sum[:], paged(uu[:]), AX.X, ALU.add)
+        ruu = f32(PAGES, "ruu")
+        nc.vector.tensor_tensor(ruu[:], uu_sum[:], r3[:], ALU.mult)
+        jn = f32(PAGES, "jn")
+        jn_sum = f32(1, "jn_sum")
+        nc.vector.scalar_tensor_tensor(jn[:], p2[:], 1.0, ruu[:], ALU.mult, ALU.subtract, accum_out=jn_sum[:])
+        e = f32(PAGES, "e")
+        nc.vector.scalar_tensor_tensor(e[:], r[:], jn_sum[:], jn[:], ALU.mult, ALU.subtract)
+
+        for half in range(HALVES):
+            cols = slice(half * width, (half + 1) * width)
+            pages = slice(half * PAGES // HALVES, (half + 1) * PAGES // HALVES)
+            s1 = f32(width, "s1_%d" % half)
+            nc.vector.scalar_tensor_tensor(s1[:], lin[:, cols], 128.0, t[:, cols], ALU.mult, ALU.mult)
+            s2 = f32(width, "s2_%d" % half)
+            nc.vector.tensor_tensor(paged(s2[:]), paged(s1[:]), spread(hn[:, pages]), ALU.add)
+            s3 = f32(width, "s3_%d" % half)
+            nc.vector.tensor_tensor(s3[:], s2[:], u[:, cols], ALU.mult)
+            s4 = f32(width, "s4_%d" % half)
+            nc.vector.tensor_tensor(s4[:], base_sb[:, cols], s3[:], ALU.subtract)
+            s5 = f32(width, "s5_%d" % half)
+            nc.vector.tensor_tensor(paged(s5[:]), paged(s4[:]), spread(e[:, pages]), ALU.add)
+            nc.sync.dma_start(out[:, cols], s5[:])

@@ -51,7 +51,7 @@ def tile_attend_gppagetimessigmoid_kernel(
             return tile
 
         def load_scales(clear, queue, scales, name):
-            tile = pool.tile([P, TOKENS], U8, name=name)
+            tile = pool.tile([P, TOKENS], U8, name=name, tag=name)
             clear.memset(tile[:].bitcast(I32), 0)
             for quad in range(4):
                 queue.dma_start(
@@ -98,44 +98,40 @@ def tile_attend_gppagetimessigmoid_kernel(
             )
             return acc
 
-        key_scale_pool = load_scales(nc.vector, nc.scalar, keys_scales, "key_scale_pool")
+        key_scale_pool = pool.tile([P, TOKENS], U8, name="key_scale_pool")
+        for quad in range(4):
+            rows = keys_scales[0, 4 * quad : 4 * quad + 4, :].bitcast(I32)
+            nc.sync.dma_start(
+                key_scale_pool[32 * quad : 32 * quad + 32, :].bitcast(I32),
+                rows.unsqueeze(0).to_broadcast([8, 4, TOKENS // 4]),
+            )
         key_word_pool = load_words(keys_words, "key_word_pool")
         query_raw = load_rows(query, "query_raw")
         val_word_pool = load_words(vals_words, "val_word_pool")
-
+        val_scale_pool = load_scales(nc.vector, nc.sync, vals_scales, "val_scale_pool")
+        gout_raw = load_rows(gout, "gout_raw")
         th_col = f32(1, "th_col")
-        nc.gpsimd.dma_start(th_col[:], th)
+        nc.sync.dma_start(th_col[:], th)
         sharp_col = f32(1, "sharp_col")
-        nc.gpsimd.dma_start(sharp_col[:], sharp)
+        nc.sync.dma_start(sharp_col[:], sharp)
+        base_sb = f32(SLOTS, "base_sb")
+        nc.sync.dma_start(base_sb[:], base)
 
-        val_scale_pool = load_scales(nc.gpsimd, nc.sync, vals_scales, "val_scale_pool")
-
-        warm = pool.tile([P, 1], F32, name="warm", tag="gout_raw")
+        warm = f32(1, "warm")
         nc.vector.memset(warm[:], 0.0)
         warm_out = f32(1, "warm_out")
         nc.scalar.activation(warm_out[:], warm[:], ACT.Exp)
-
-        query_grouped = interleave(query_raw, "query_grouped")
-        gout_raw = load_rows(gout, "gout_raw")
-
-        key_scales = gather(key_scale_pool, offsets[:], U8, "key_scales")
-        key_words = gather(key_word_pool, offsets[:], U16, "key_words")
-        q_codes, q_scales = quantise(query_grouped, "query")
-        a = product(q_codes, q_scales, key_words[:], key_scales[:], "a")
-
-        base_sb = pool.tile([P, SLOTS], F32, name="base_sb", tag="key_word_pool")
-        nc.sync.dma_start(base_sb[:], base)
 
         def row_factor(col, factor, name):
             tile = f32(1, name)
             nc.scalar.mul(tile[:], col[:], factor)
             return tile
 
-        th_bias = row_factor(th_col, -0.5, "th_bias")
-        neg_k = row_factor(sharp_col, -1.0 / 16.0, "neg_k")
-        kappa_k = row_factor(sharp_col, -1.0 / 8.0, "kappa_k")
-        r3_k = row_factor(sharp_col, 8.0, "r3_k")
-        g_k = row_factor(sharp_col, 128.0, "g_k")
+        query_grouped = interleave(query_raw, "query_grouped")
+        key_scales = gather(key_scale_pool, offsets[:], U8, "key_scales")
+        key_words = gather(key_word_pool, offsets[:], U16, "key_words")
+        q_codes, q_scales = quantise(query_grouped, "query")
+        a = product(q_codes, q_scales, key_words[:], key_scales[:], "a")
 
         gout_grouped = interleave(gout_raw, "gout_grouped")
         val_words = gather(val_word_pool, offsets[:], U16, "val_words")
@@ -148,10 +144,16 @@ def tile_attend_gppagetimessigmoid_kernel(
             val_scales = gather(val_scale_pool, offsets[:, pages], U8, "val_scales_%d" % half)
             c.append(product(g_codes, g_scales, val_words[:, cols], val_scales[:], "c_%d" % half))
 
+        th_bias = row_factor(th_col, -0.5, "th_bias")
         t = f32(SLOTS, "t")
         nc.scalar.activation(t[:], a[:], ACT.Tanh, bias=th_bias[:], scale=0.5)
         tt = f32(SLOTS, "tt")
         nc.scalar.activation(tt[:], t[:], ACT.Square)
+
+        neg_k = row_factor(sharp_col, -1.0 / 16.0, "neg_k")
+        kappa_k = row_factor(sharp_col, -1.0 / 8.0, "kappa_k")
+        r3_k = row_factor(sharp_col, 8.0, "r3_k")
+        g_k = row_factor(sharp_col, 128.0, "g_k")
 
         a_sum = f32(PAGES, "a_sum")
         nc.vector.tensor_reduce(a_sum[:], paged(a[:]), AX.X, ALU.add)
@@ -161,7 +163,7 @@ def tile_attend_gppagetimessigmoid_kernel(
         p = f32(PAGES, "p")
         z = f32(1, "z")
         nc.scalar.activation(p[:], neg_s[:], ACT.Exp, bias=neg_max[:], scale=-1.0, accum_out=z[:])
-        inv_z = f32(1, "inv_z")
+        inv_z = pool.tile([P, 1], F32, name="inv_z", tag="val_scale_pool")
         nc.vector.reciprocal(inv_z[:], z[:])
         r = f32(PAGES, "r")
         nc.scalar.activation(r[:], p[:], ACT.Identity, scale=inv_z[:])
@@ -169,6 +171,11 @@ def tile_attend_gppagetimessigmoid_kernel(
         nc.scalar.activation(r2[:], p[:], ACT.Square, scale=inv_z[:])
         r3 = f32(PAGES, "r3")
         nc.scalar.activation(r3[:], r2[:], ACT.Identity, scale=r3_k[:])
+
+        zt = f32(width, "zt")
+        for g in range(PAGES // HALVES):
+            cols = slice(g * PAGE, (g + 1) * PAGE)
+            nc.scalar.activation(zt[:, cols], t[:, cols], ACT.Identity, scale=r2[:, g : g + 1])
 
         u = f32(SLOTS, "u")
         w = f32(SLOTS, "w")
@@ -190,7 +197,7 @@ def tile_attend_gppagetimessigmoid_kernel(
         nc.vector.tensor_tensor(beta[:], kappa[:], r2[:], ALU.mult)
 
         lin = f32(SLOTS, "lin")
-        for g in range(PAGES):
+        for g in range(PAGES // HALVES, PAGES):
             cols = slice(g * PAGE, (g + 1) * PAGE)
             nc.scalar.activation(
                 lin[:, cols], u[:, cols], ACT.Identity, bias=beta[:, g : g + 1], scale=r2[:, g : g + 1]
@@ -223,7 +230,12 @@ def tile_attend_gppagetimessigmoid_kernel(
             cols = slice(half * width, (half + 1) * width)
             pages = slice(half * PAGES // HALVES, (half + 1) * PAGES // HALVES)
             s1 = f32(width, "s1_%d" % half)
-            nc.vector.scalar_tensor_tensor(s1[:], lin[:, cols], 128.0, t[:, cols], ALU.mult, ALU.mult)
+            if half == 0:
+                y = f32(width, "y")
+                nc.vector.tensor_tensor(paged(y[:]), paged(u[:, cols]), spread(kappa[:, pages]), ALU.add)
+                nc.vector.scalar_tensor_tensor(s1[:], y[:], 128.0, zt[:], ALU.mult, ALU.mult)
+            else:
+                nc.vector.scalar_tensor_tensor(s1[:], lin[:, cols], 128.0, t[:, cols], ALU.mult, ALU.mult)
             s2 = f32(width, "s2_%d" % half)
             nc.vector.tensor_tensor(paged(s2[:]), paged(s1[:]), spread(hn[:, pages]), ALU.add)
             s3 = f32(width, "s3_%d" % half)

@@ -53,20 +53,17 @@ def tile_attend_gppagetimessigmoid_kernel(
         def load_scales(clear, queue, scales, name):
             tile = pool.tile([P, TOKENS], U8, name=name, tag=name)
             clear.memset(tile[:].bitcast(I32), 0)
-            for quad in range(4):
-                queue.dma_start(
-                    tile[32 * quad : 32 * quad + 4, :].bitcast(I32),
-                    scales[0, 4 * quad : 4 * quad + 4, :].bitcast(I32),
-                )
+            for row in range(4):
+                queue.dma_start(tile[row:P:32, :].bitcast(I32), scales[0, row:16:4, :].bitcast(I32))
             return tile
 
         def load_rows(rows, name):
-            raw = pool.tile([P, PACK, P], F32, name=name, tag=name)
+            raw = pool.tile([P, PACK, P], F32, name=name, tag="raw_rows")
             nc.sync.dma_start(raw[:], rows.rearrange("(p j) q -> p j q", j=PACK))
             return raw
 
         def interleave(raw, name):
-            grouped = pool.tile([P, P, PACK], BF16, name=name, align_bytes=64)
+            grouped = pool.tile([P, P, PACK], BF16, name=name, tag=name, align_bytes=64)
             nc.scalar.copy(grouped[:], raw[:].rearrange("p j q -> p q j"))
             return grouped
 
@@ -98,56 +95,51 @@ def tile_attend_gppagetimessigmoid_kernel(
             )
             return acc
 
-        key_scale_pool = pool.tile([P, TOKENS], U8, name="key_scale_pool")
-        for quad in range(4):
-            rows = keys_scales[0, 4 * quad : 4 * quad + 4, :].bitcast(I32)
-            nc.sync.dma_start(
-                key_scale_pool[32 * quad : 32 * quad + 32, :].bitcast(I32),
-                rows.unsqueeze(0).to_broadcast([8, 4, TOKENS // 4]),
-            )
         key_word_pool = load_words(keys_words, "key_word_pool")
+        key_scale_pool = load_scales(nc.vector, nc.sync, keys_scales, "key_scale_pool")
         query_raw = load_rows(query, "query_raw")
-        val_word_pool = load_words(vals_words, "val_word_pool")
-        val_scale_pool = load_scales(nc.vector, nc.sync, vals_scales, "val_scale_pool")
-        gout_raw = load_rows(gout, "gout_raw")
         th_col = f32(1, "th_col")
         nc.sync.dma_start(th_col[:], th)
-        sharp_col = f32(1, "sharp_col")
-        nc.sync.dma_start(sharp_col[:], sharp)
-        base_sb = f32(SLOTS, "base_sb")
-        nc.sync.dma_start(base_sb[:], base)
 
-        warm = f32(1, "warm")
+        warm = pool.tile([P, 1], F32, name="warm", tag="val_scale_pool")
         nc.vector.memset(warm[:], 0.0)
-        warm_out = f32(1, "warm_out")
+        warm_out = pool.tile([P, 1], F32, name="warm_out", tag="val_word_pool")
         nc.scalar.activation(warm_out[:], warm[:], ACT.Exp)
+
+        val_word_pool = load_words(vals_words, "val_word_pool")
+        val_scale_pool = load_scales(nc.vector, nc.sync, vals_scales, "val_scale_pool")
 
         def row_factor(col, factor, name):
             tile = f32(1, name)
             nc.scalar.mul(tile[:], col[:], factor)
             return tile
 
+        th_bias = row_factor(th_col, -0.5, "th_bias")
         query_grouped = interleave(query_raw, "query_grouped")
-        key_scales = gather(key_scale_pool, offsets[:], U8, "key_scales")
+        gout_raw = load_rows(gout, "gout_raw")
         key_words = gather(key_word_pool, offsets[:], U16, "key_words")
+        key_scales = gather(key_scale_pool, offsets[:], U8, "key_scales")
         q_codes, q_scales = quantise(query_grouped, "query")
         a = product(q_codes, q_scales, key_words[:], key_scales[:], "a")
 
+        sharp_col = pool.tile([P, 1], F32, name="sharp_col", tag="key_word_pool")
+        nc.sync.dma_start(sharp_col[:], sharp)
+        base_sb = pool.tile([P, SLOTS], F32, name="base_sb", tag="query_grouped", align_bytes=64)
+        nc.sync.dma_start(base_sb[:], base)
+
         gout_grouped = interleave(gout_raw, "gout_grouped")
         val_words = gather(val_word_pool, offsets[:], U16, "val_words")
+        val_scales = gather(val_scale_pool, offsets[:], U8, "val_scales")
         g_codes, g_scales = quantise(gout_grouped, "gout")
         width = SLOTS // HALVES
         c = []
         for half in range(HALVES):
             cols = slice(half * width, (half + 1) * width)
-            pages = slice(half * PAGES // HALVES, (half + 1) * PAGES // HALVES)
-            val_scales = gather(val_scale_pool, offsets[:, pages], U8, "val_scales_%d" % half)
-            c.append(product(g_codes, g_scales, val_words[:, cols], val_scales[:], "c_%d" % half))
+            c.append(product(g_codes, g_scales, val_words[:, cols], val_scales[:, cols], "c_%d" % half))
 
-        th_bias = row_factor(th_col, -0.5, "th_bias")
         t = f32(SLOTS, "t")
         nc.scalar.activation(t[:], a[:], ACT.Tanh, bias=th_bias[:], scale=0.5)
-        tt = f32(SLOTS, "tt")
+        tt = pool.tile([P, SLOTS], F32, name="tt", tag="raw_rows")
         nc.scalar.activation(tt[:], t[:], ACT.Square)
 
         neg_k = row_factor(sharp_col, -1.0 / 16.0, "neg_k")
@@ -155,7 +147,7 @@ def tile_attend_gppagetimessigmoid_kernel(
         r3_k = row_factor(sharp_col, 8.0, "r3_k")
         g_k = row_factor(sharp_col, 128.0, "g_k")
 
-        a_sum = f32(PAGES, "a_sum")
+        a_sum = pool.tile([P, PAGES], F32, name="a_sum", tag="gout_grouped", align_bytes=64)
         nc.vector.tensor_reduce(a_sum[:], paged(a[:]), AX.X, ALU.add)
         neg_s = f32(PAGES, "neg_s")
         neg_max = f32(1, "neg_max")
@@ -163,7 +155,7 @@ def tile_attend_gppagetimessigmoid_kernel(
         p = f32(PAGES, "p")
         z = f32(1, "z")
         nc.scalar.activation(p[:], neg_s[:], ACT.Exp, bias=neg_max[:], scale=-1.0, accum_out=z[:])
-        inv_z = pool.tile([P, 1], F32, name="inv_z", tag="val_scale_pool")
+        inv_z = f32(1, "inv_z")
         nc.vector.reciprocal(inv_z[:], z[:])
         r = f32(PAGES, "r")
         nc.scalar.activation(r[:], p[:], ACT.Identity, scale=inv_z[:])

from contextlib import ExitStack

import concourse.mybir as mybir

F32 = mybir.dt.float32
BF16 = mybir.dt.bfloat16
I32 = mybir.dt.int32
U32 = mybir.dt.uint32
U16 = mybir.dt.uint16
U8 = mybir.dt.uint8
FP8X4 = mybir.dt.float8_e4m3fn_x4
FP4X4 = mybir.dt.float4_e2m1fn_x4
ALU = mybir.AluOpType
ACT = mybir.ActivationFunctionType
AX = mybir.AxisListType

P = 128
PACK = 4
TOKENS = 2048
SLOTS = 512
PAGES = 32
PAGE = 16
HALVES = 2

FLOPS = 2 * 2 * 512 * P * SLOTS


def tile_attend_gppagetimessigmoid_kernel(
    tc, query, keys_words, keys_scales, th, sharp, gout, vals_words, vals_scales, base, offs, out
):
    nc = tc.nc
    with ExitStack() as ctx:
        pool = ctx.enter_context(tc.tile_pool(name="sbuf", bufs=1))
        psum = ctx.enter_context(tc.psum_pool(name="psum", bufs=1))

        def f32(width, name):
            return pool.tile([P, width], F32, name=name)

        def paged(ap):
            return ap.rearrange("p (g j) -> p g j", j=PAGE)

        def spread(ap):
            return ap.unsqueeze(2).to_broadcast([P, ap.shape[1], PAGE])

        offsets = pool.tile([P, SLOTS // 16], U16, name="offsets")
        nc.sync.dma_start(offsets[:], offs)

        def load_words(words, name):
            tile = pool.tile([P, TOKENS], U16, name=name, tag=name)
            nc.sync.dma_start(tile[:].bitcast(I32), words[0].bitcast(I32))
            return tile

        def load_scales(clear, queue, scales, name):
            tile = pool.tile([P, TOKENS], U8, name=name, tag=name)
            clear.memset(tile[:].bitcast(I32), 0)
            for row in range(4):
                queue.dma_start(tile[row:P:32, :].bitcast(I32), scales[0, row:16:4, :].bitcast(I32))
            return tile

        def load_rows(rows, name):
            raw = pool.tile([P, PACK, P], F32, name=name, tag="raw_rows")
            nc.sync.dma_start(raw[:], rows.rearrange("(p j) q -> p j q", j=PACK))
            return raw

        def interleave(raw, name):
            grouped = pool.tile([P, P, PACK], BF16, name=name, tag=name, align_bytes=64)
            nc.scalar.copy(grouped[:], raw[:].rearrange("p j q -> p q j"))
            return grouped

        def quantise(grouped, name):
            codes = pool.tile([P, P], U32, name=name + "_codes", align_bytes=64)
            scales = pool.tile([P, P], U8, name=name + "_scales", align_bytes=64)
            nc.vector.quantize_mx(
                out=codes[:].bitcast(FP8X4),
                scales=scales[:],
                in_=grouped[:].rearrange("p q j -> p (q j)"),
            )
            return codes, scales

        def gather(window, entries, dtype, name):
            picked = pool.tile([P, 16 * entries.shape[1]], dtype, name=name, align_bytes=64)
            nc.vector.tensor_copy(picked[:], window[:].indirect(entries))
            return picked

        def product(codes, scales, words, word_scales, name):
            acc = psum.tile([P, words.shape[1]], F32, name=name)
            nc.tensor.matmul_mx(
                out=acc[:],
                lhsT=codes[:].bitcast(FP8X4),
                lhsT_scale=scales[:],
                rhs=words.bitcast(FP4X4),
                rhs_scale=word_scales,
                start=True,
                stop=True,
            )
            return acc

        key_word_pool = load_words(keys_words, "key_word_pool")
        key_scale_pool = load_scales(nc.vector, nc.sync, keys_scales, "key_scale_pool")
        query_raw = load_rows(query, "query_raw")
        th_col = f32(1, "th_col")
        nc.sync.dma_start(th_col[:], th)

        warm = pool.tile([P, 1], F32, name="warm", tag="val_scale_pool")
        nc.vector.memset(warm[:], 0.0)
        warm_out = pool.tile([P, 1], F32, name="warm_out", tag="val_word_pool")
        nc.scalar.activation(warm_out[:], warm[:], ACT.Exp)

        val_word_pool = load_words(vals_words, "val_word_pool")
        val_scale_pool = load_scales(nc.vector, nc.sync, vals_scales, "val_scale_pool")

        def row_factor(col, factor, name):
            tile = f32(1, name)
            nc.scalar.mul(tile[:], col[:], factor)
            return tile

        th_bias = row_factor(th_col, -0.5, "th_bias")
        query_grouped = interleave(query_raw, "query_grouped")
        gout_raw = load_rows(gout, "gout_raw")
        key_words = gather(key_word_pool, offsets[:], U16, "key_words")
        key_scales = gather(key_scale_pool, offsets[:], U8, "key_scales")
        q_codes, q_scales = quantise(query_grouped, "query")
        a = product(q_codes, q_scales, key_words[:], key_scales[:], "a")

        sharp_col = pool.tile([P, 1], F32, name="sharp_col", tag="key_word_pool")
        nc.sync.dma_start(sharp_col[:], sharp)
        base_sb = pool.tile([P, SLOTS], F32, name="base_sb", tag="query_grouped", align_bytes=64)
        nc.sync.dma_start(base_sb[:], base)

        gout_grouped = interleave(gout_raw, "gout_grouped")
        val_words = gather(val_word_pool, offsets[:], U16, "val_words")
        val_scales = gather(val_scale_pool, offsets[:], U8, "val_scales")
        g_codes, g_scales = quantise(gout_grouped, "gout")
        width = SLOTS // HALVES
        c = []
        for half in range(HALVES):
            cols = slice(half * width, (half + 1) * width)
            c.append(product(g_codes, g_scales, val_words[:, cols], val_scales[:, cols], "c_%d" % half))

        t = f32(SLOTS, "t")
        nc.scalar.activation(t[:], a[:], ACT.Tanh, bias=th_bias[:], scale=0.5)
        tt = pool.tile([P, SLOTS], F32, name="tt", tag="raw_rows")
        nc.scalar.activation(tt[:], t[:], ACT.Square)

        neg_k = row_factor(sharp_col, -1.0 / 16.0, "neg_k")
        kappa_k = row_factor(sharp_col, -1.0 / 8.0, "kappa_k")
        r3_k = row_factor(sharp_col, 8.0, "r3_k")
        g_k = row_factor(sharp_col, 128.0, "g_k")

        a_sum = pool.tile([P, PAGES], F32, name="a_sum", tag="gout_grouped", align_bytes=64)
        nc.vector.tensor_reduce(a_sum[:], paged(a[:]), AX.X, ALU.add)
        neg_s = f32(PAGES, "neg_s")
        neg_max = f32(1, "neg_max")
        nc.vector.tensor_scalar(neg_s[:], a_sum[:], neg_k[:], None, ALU.mult, ALU.min, accum_out=neg_max[:])
        p = f32(PAGES, "p")
        z = f32(1, "z")
        nc.scalar.activation(p[:], neg_s[:], ACT.Exp, bias=neg_max[:], scale=-1.0, accum_out=z[:])
        inv_z = f32(1, "inv_z")
        nc.vector.reciprocal(inv_z[:], z[:])
        r = f32(PAGES, "r")
        nc.scalar.activation(r[:], p[:], ACT.Identity, scale=inv_z[:])
        r2 = f32(PAGES, "r2")
        nc.scalar.activation(r2[:], p[:], ACT.Square, scale=inv_z[:])
        r3 = f32(PAGES, "r3")
        nc.scalar.activation(r3[:], r2[:], ACT.Identity, scale=r3_k[:])

        zt = f32(width, "zt")
        for g in range(PAGES // HALVES):
            cols = slice(g * PAGE, (g + 1) * PAGE)
            nc.scalar.activation(zt[:, cols], t[:, cols], ACT.Identity, scale=r2[:, g : g + 1])

        u = f32(SLOTS, "u")
        w = f32(SLOTS, "w")
        for half in range(HALVES):
            cols = slice(half * width, (half + 1) * width)
            nc.vector.scalar_tensor_tensor(w[:, cols], t[:, cols], 1.0, c[half][:], ALU.add, ALU.mult)
            nc.vector.scalar_tensor_tensor(u[:, cols], tt[:, cols], -1.0, c[half][:], ALU.add, ALU.mult)
        uu = f32(SLOTS, "uu")
        nc.scalar.activation(uu[:], u[:], ACT.Square)

        w_sum = f32(PAGES, "w_sum")
        nc.vector.tensor_reduce(w_sum[:], paged(w[:]), AX.X, ALU.add)
        rw = f32(PAGES, "rw")
        w_mean = f32(1, "w_mean")
        nc.vector.scalar_tensor_tensor(rw[:], w_sum[:], 1.0, r[:], ALU.mult, ALU.mult, accum_out=w_mean[:])
        kappa = f32(PAGES, "kappa")
        nc.vector.tensor_scalar(kappa[:], w_sum[:], w_mean[:], kappa_k[:], ALU.subtract, ALU.mult)
        beta = f32(PAGES, "beta")
        nc.vector.tensor_tensor(beta[:], kappa[:], r2[:], ALU.mult)

        lin = f32(SLOTS, "lin")
        for g in range(PAGES // HALVES, PAGES):
            cols = slice(g * PAGE, (g + 1) * PAGE)
            nc.scalar.activation(
                lin[:, cols], u[:, cols], ACT.Identity, bias=beta[:, g : g + 1], scale=r2[:, g : g + 1]
            )

        u_sum = f32(PAGES, "u_sum")
        nc.vector.tensor_reduce(u_sum[:], paged(u[:]), AX.X, ALU.add)
        ru = f32(PAGES, "ru")
        nc.vector.tensor_tensor(ru[:], u_sum[:], r3[:], ALU.mult)
        g1 = f32(PAGES, "g1")
        g_sum = f32(1, "g_sum")
        nc.vector.scalar_tensor_tensor(g1[:], beta[:], g_k[:], ru[:], ALU.mult, ALU.add, accum_out=g_sum[:])
        hn = f32(PAGES, "hn")
        nc.vector.scalar_tensor_tensor(hn[:], r[:], g_sum[:], g1[:], ALU.mult, ALU.subtract)
        p1 = f32(PAGES, "p1")
        nc.vector.tensor_tensor(p1[:], hn[:], ru[:], ALU.subtract)
        p2 = f32(PAGES, "p2")
        nc.vector.tensor_tensor(p2[:], p1[:], kappa[:], ALU.mult)
        uu_sum = f32(PAGES, "uu_sum")
        nc.vector.tensor_reduce(uu_sum[:], paged(uu[:]), AX.X, ALU.add)
        ruu = f32(PAGES, "ruu")
        nc.vector.tensor_tensor(ruu[:], uu_sum[:], r3[:], ALU.mult)
        jn = f32(PAGES, "jn")
        jn_sum = f32(1, "jn_sum")
        nc.vector.scalar_tensor_tensor(jn[:], p2[:], 1.0, ruu[:], ALU.mult, ALU.subtract, accum_out=jn_sum[:])
        e = f32(PAGES, "e")
        nc.vector.scalar_tensor_tensor(e[:], r[:], jn_sum[:], jn[:], ALU.mult, ALU.subtract)

        for half in range(HALVES):
            cols = slice(half * width, (half + 1) * width)
            pages = slice(half * PAGES // HALVES, (half + 1) * PAGES // HALVES)
            s1 = f32(width, "s1_%d" % half)
            if half == 0:
                y = f32(width, "y")
                nc.vector.tensor_tensor(paged(y[:]), paged(u[:, cols]), spread(kappa[:, pages]), ALU.add)
                nc.vector.scalar_tensor_tensor(s1[:], y[:], 128.0, zt[:], ALU.mult, ALU.mult)
            else:
                nc.vector.scalar_tensor_tensor(s1[:], lin[:, cols], 128.0, t[:, cols], ALU.mult, ALU.mult)
            s2 = f32(width, "s2_%d" % half)
            nc.vector.tensor_tensor(paged(s2[:]), paged(s1[:]), spread(hn[:, pages]), ALU.add)
            s3 = f32(width, "s3_%d" % half)
            nc.vector.tensor_tensor(s3[:], s2[:], u[:, cols], ALU.mult)
            s4 = f32(width, "s4_%d" % half)
            nc.vector.tensor_tensor(s4[:], base_sb[:, cols], s3[:], ALU.subtract)
            s5 = f32(width, "s5_%d" % half)
            nc.vector.tensor_tensor(paged(s5[:]), paged(s4[:]), spread(e[:, pages]), ALU.add)
            nc.sync.dma_start(out[:, cols], s5[:])
